import numpy as np
import ml_dtypes


def mxq(x, axis, fmt="e4m3"):
    dtype, down = {"e4m3": (ml_dtypes.float8_e4m3fn, 7), "e5m2": (ml_dtypes.float8_e5m2, 14)}[fmt]
    v = np.moveaxis(np.asarray(x, np.float32).astype(ml_dtypes.bfloat16).astype(np.float64), axis, -1)
    blocks = v.reshape(v.shape[:-1] + (-1, 32))
    amax = np.abs(blocks).max(-1, keepdims=True)
    byte = np.maximum(np.where(amax > 0, np.frexp(amax)[1] - 1 + 127, 0) - down, 1)
    scale = np.exp2(byte - 127.0)
    codes = (blocks / scale).astype(np.float32).astype(dtype).astype(np.float64)
    return np.moveaxis((codes * scale).reshape(v.shape), -1, axis)


WIDE = False


def mx_kscale(k):
    if not WIDE:
        return np.ones(k)
    levels = np.array([24, -24, 12, -12, 0])
    if k % 512:
        return np.exp2(np.random.permutation(np.resize(levels, k // 32))).repeat(32)
    a = np.empty((k // 512, 16))
    for p in range(k // 512):
        a[p, :8] = np.random.permutation(np.resize(levels, 8))
        for g in range(8):
            far = levels[np.abs(levels - a[p, g]) >= 10]
            a[p, g + 8] = far[np.random.randint(len(far))]
    return np.exp2(a.ravel()).repeat(32)


def f64(x):
    return np.asarray(x).astype(np.float64)


def striped(idx):
    return np.tile(idx.reshape(-1, 16).T, (8, 1)).astype(np.uint16)


def unstriped(offs):
    return offs[:16].T.reshape(-1).astype(np.int64)


E2M1 = np.array([0.0, 0.5, 1.0, 1.5, 2.0, 3.0, 4.0, 6.0, -0.0, -0.5, -1.0, -1.5, -2.0, -3.0, -4.0, -6.0])


def pack_weight(w, fmt):
    k, n = w.shape
    w = f64(np.asarray(w, np.float32).astype(ml_dtypes.bfloat16)).reshape(k // 32, 32, n)
    amax = np.abs(w).max(1)
    if fmt == "e4m3":
        byte = np.frexp(amax)[1] - 1 + 127 - 7
    else:
        mant, ex = np.frexp(amax / 6.0)
        byte = np.where(mant > 0.5, ex, ex - 1) + 127
    byte = np.clip(np.where(amax > 0, byte, 1), 1, 254)
    scaled = (w * np.exp2(127.0 - byte)[:, None, :]).reshape(k, n).astype(np.float32)
    by_word = np.ascontiguousarray(scaled.reshape(k // 512, 128, 4, n).transpose(0, 1, 3, 2))
    if fmt == "e4m3":
        words = by_word.astype(ml_dtypes.float8_e4m3fn).view(np.uint8)
    else:
        c = by_word.astype(ml_dtypes.float4_e2m1fn).view(np.uint8) & 0xF
        words = (c[..., 0::2] | (c[..., 1::2] << 4)).reshape(k // 512, 128, 2 * n)
    return np.ascontiguousarray(words), np.ascontiguousarray(byte.astype(np.uint8).reshape(k // 512, 16, n))


def unpack_weight(words, scales, fmt):
    g, _, n = scales.shape
    words = np.ascontiguousarray(words).reshape(g, 128, n, -1)
    if fmt == "e4m3":
        vals = words.view(ml_dtypes.float8_e4m3fn).astype(np.float64)
    else:
        nib = np.empty((g, 128, n, 4), np.uint8)
        nib[..., 0::2] = words & 0xF
        nib[..., 1::2] = words >> 4
        vals = E2M1[nib]
    vals = vals * np.repeat(np.exp2(scales.astype(np.float64) - 127.0), 8, axis=1)[..., None]
    return vals.transpose(0, 1, 3, 2).reshape(g * 512, n)


def pack_table4(v):
    words, scales = pack_weight(v, "e2m1")
    g, t = words.shape[0] // 2, v.shape[1]
    return np.ascontiguousarray(words.reshape(g, 2, 128, t, 2).transpose(0, 2, 3, 1, 4).reshape(g, 128, t, 4)), scales


def unpack_table4(words, scales):
    g, _, t, _ = words.shape
    return unpack_weight(words.reshape(g, 128, t, 2, 2).transpose(0, 3, 1, 2, 4).reshape(2 * g, 128, 2 * t), scales, "e2m1")


K, L, R, N, T, J = 512, 1024, 1024, 1024, 2048, 1024


def setup_inputs():
    n = np.random.standard_normal
    s = mx_kscale(K)[:, None]
    s2 = mx_kscale(L)[:, None]
    u = mx_kscale(R)[:, None]
    en = n((R, N)) / np.sqrt(R) / u
    p_tab = pack_weight(n((K, T)) * s, "e4m3")
    p_tab2 = pack_table4(n((L, T)) * s2)
    p_wa = pack_weight(n((K, R)) / np.sqrt(K) / s, "e2m1")
    p_wb = pack_weight(n((L, R)) / np.sqrt(L) / s2, "e4m3")
    p_en8 = pack_weight(en[:512], "e4m3")
    p_en4 = pack_weight(en[512:], "e2m1")
    return {
        "tab_words": p_tab[0],
        "tab_scales": p_tab[1],
        "tab2_words": p_tab2[0],
        "tab2_scales": p_tab2[1],
        "wa_words": p_wa[0],
        "wa_scales": p_wa[1],
        "wb_words": p_wb[0],
        "wb_scales": p_wb[1],
        "sm": (np.random.uniform(0.5, 2.0, R) * u[:, 0]).astype(np.float32),
        "en8_words": p_en8[0],
        "en8_scales": p_en8[1],
        "en4_words": p_en4[0],
        "en4_scales": p_en4[1],
        "b": (0.3 * n(N)).astype(np.float32),
        "offs": striped(np.random.permutation(T)[:J]),
        "offs2": striped(np.random.permutation(T)[:J]),
    }


def reference(tab_words, tab_scales, tab2_words, tab2_scales, wa_words, wa_scales, wb_words, wb_scales, sm, en8_words, en8_scales, en4_words, en4_scales, b, offs, offs2):
    idx = unstriped(offs)
    idx2 = unstriped(offs2)
    tab_ = unpack_weight(tab_words, tab_scales, "e4m3")[:, idx]
    tab2_ = unpack_table4(tab2_words, tab2_scales)[:, idx2]
    wa_ = unpack_weight(wa_words, wa_scales, "e2m1")
    wb_ = unpack_weight(wb_words, wb_scales, "e4m3")
    z = wa_.T @ tab_ + wb_.T @ tab2_
    h = f64(sm)[:, None] * np.tanh(z)
    h_ = mxq(h, 0, "e4m3")
    en8_ = unpack_weight(en8_words, en8_scales, "e4m3")
    en4_ = unpack_weight(en4_words, en4_scales, "e2m1")
    y = en8_.T @ h_[:512] + en4_.T @ h_[512:]
    return y + f64(b)[:, None]

@@ -1,0 +1,254 @@
+from contextlib import ExitStack
+
+import concourse.mybir as mybir
+
+K, L, R, N, T, J = 512, 1024, 1024, 1024, 2048, 1024
+FLOPS = 2 * J * (K * R + L * R + R * N)
+
+F32 = mybir.dt.float32
+BF16 = mybir.dt.bfloat16
+I32 = mybir.dt.int32
+U32 = mybir.dt.uint32
+U16 = mybir.dt.uint16
+U8 = mybir.dt.uint8
+FP8X4 = mybir.dt.float8_e4m3fn_x4
+FP4X4 = mybir.dt.float4_e2m1fn_x4
+ACT = mybir.ActivationFunctionType
+ALU = mybir.AluOpType
+
+P = 128
+PACK = 4
+PASS = P * PACK
+CHUNK = 512
+PIECE = 256
+QUADS = 4
+LIFT = 4
+LIVE = 100
+
+
+def tile_list_kg_tanh_mix_bias_kernel(
+    tc, tab_words, tab_scales, tab2_words, tab2_scales, wa_words, wa_scales, wb_words, wb_scales,
+    sm, en8_words, en8_scales, en4_words, en4_scales, b, offs, offs2, out,
+):
+    nc = tc.nc
+    with ExitStack() as ctx:
+        keep = ctx.enter_context(tc.tile_pool(name="keep", bufs=1))
+        psum = ctx.enter_context(tc.psum_pool(name="psum", bufs=1))
+
+        def sb(shape, dtype, name, tag=None):
+            return keep.tile(shape, dtype, name=name, tag=tag or name, align_bytes=64)
+
+        def bank(i, name):
+            return psum.tile([P, 512], F32, name=name, tag="bank%d" % i)
+
+        def zero(tile_ap):
+            nc.vector.memset(tile_ap.bitcast(I32), 0)
+
+        def load_plane(queues, plane, rows):
+            for q in range(QUADS):
+                queues[q].dma_start(out=plane[32 * q : 32 * q + 4, :].bitcast(I32), in_=rows[4 * q : 4 * q + 4, :].bitcast(I32))
+
+        def load_repeated(queues, plane, rows):
+            width = rows.shape[1] // 4
+            for q in range(QUADS):
+                four = rows[4 * q : 4 * q + 4, :].bitcast(I32)
+                queues[q].dma_start(out=plane[32 * q : 32 * q + 32, :].bitcast(I32), in_=four.unsqueeze(0).to_broadcast([8, 4, width]))
+
+        list1 = keep.tile([P, J // 16], U16, name="list1")
+        list2 = keep.tile([P, J // 16], U16, name="list2")
+
+        tab_s = sb([P, T], U8, "tab_s")
+        tab_w = sb([P, T], I32, "tab_w")
+        tab2_s = sb([P, T], U8, "tab2_s")
+        tab2_w = sb([P, T], I32, "tab2_w")
+        wa_s_raw = sb([P, R], U8, "wa_s_raw")
+        wa_w_raw = sb([P, 2 * R], U8, "wa_w_raw")
+        wb_s_raw = sb([P, 2 * R], U8, "wb_s_raw")
+        wb_w_raw = [sb([P, 2, PASS], I32, "wb_w_raw%d" % g) for g in range(2)]
+        en8_s = sb([P, N], U8, "en8_s")
+        en8_w = sb([P, N], I32, "en8_w")
+        en4_s = sb([P, N], U8, "en4_s")
+        en4_w = sb([P, 2 * N], U8, "en4_w")
+        sm_t = sb([P, 2, PACK], F32, "sm_t")
+        b_t = sb([P, N // P], F32, "b_t")
+        s2_second = [sb([P, CHUNK], U8, "s2_second%d" % c) for c in range(2)]
+
+        for tl in (tab2_s, wb_s_raw, s2_second[0], s2_second[1], en8_s, en4_s):
+            zero(tl[:])
+
+        nc.sync.dma_start(list1[:], offs)
+        load_repeated([nc.sync] * 4, tab_s, tab_scales[0])
+        load_repeated([nc.sync, nc.sync, nc.gpsimd, nc.gpsimd], wa_s_raw, wa_scales[0])
+        nc.sync.dma_start(out=tab_w[:], in_=tab_words[0].rearrange("p n t -> p (n t)").bitcast(I32))
+        nc.sync.dma_start(out=wa_w_raw[:].bitcast(I32), in_=wa_words[0].bitcast(I32))
+        nc.sync.dma_start(list2[:], offs2)
+        for q in range(QUADS):
+            nc.sync.dma_start(out=tab2_s[32 * q : 32 * q + 8, :].bitcast(I32), in_=tab2_scales[:, 4 * q : 4 * q + 4, :].bitcast(I32))
+        nc.sync.dma_start(out=tab2_w[:], in_=tab2_words[0].rearrange("p n t -> p (n t)").bitcast(I32))
+        wb_rows = wb_words.rearrange("a p n t -> p a (n t)").bitcast(I32)
+        nc.sync.dma_start(out=wb_w_raw[0][:], in_=wb_rows[:, :, 0:PASS])
+        for q in range(QUADS):
+            nc.sync.dma_start(
+                out=wb_s_raw[32 * q : 32 * q + 4, :].bitcast(I32).rearrange("p (a n) -> p a n", a=2),
+                in_=wb_scales[:, 4 * q : 4 * q + 4, :].bitcast(I32).rearrange("a r n -> r a n"),
+            )
+        nc.sync.dma_start(out=wb_w_raw[1][:], in_=wb_rows[:, :, PASS : 2 * PASS])
+        nc.sync.dma_start(out=sm_t[:], in_=sm.rearrange("(g p t) -> p g t", g=2, t=PACK))
+        nc.sync.dma_start(out=en8_w[:], in_=en8_words[0].rearrange("p n t -> p (n t)").bitcast(I32))
+        nc.sync.dma_start(out=en4_w[:].bitcast(I32), in_=en4_words[0].bitcast(I32))
+        load_plane([nc.sync] * 4, en8_s, en8_scales[0])
+        load_plane([nc.sync] * 4, en4_s, en4_scales[0])
+        with nc.allow_non_contiguous_dma(reason="one bias value a partition"):
+            nc.sync.dma_start(out=b_t[:], in_=b.rearrange("(m p) -> p m", p=P))
+
+        wa_s = sb([P, R], U8, "wa_s")
+        wa_w = [sb([P, PASS], U16, "wa_w%d" % g) for g in range(2)]
+        wb_s = [sb([P, 2, PASS], U8, "wb_s%d" % g) for g in range(2)]
+        wb_w = {(a, g): sb([P, PASS], I32, "wb_w%d%d" % (a, g)) for g in range(2) for a in range(2)}
+
+        def gather(dst, window, lst, c):
+            cols = slice(c * CHUNK // 16, (c + 1) * CHUNK // 16)
+            nc.vector.tensor_copy(dst, window.indirect(lst[:, cols]))
+
+        def deal_bytes(dst, src):
+            nc.vector.tensor_copy(
+                out=dst.rearrange("p g (t m) -> p g t m", t=PACK),
+                in_=src.rearrange("p g (m t) -> p g t m", t=PACK),
+            )
+
+        def deal_words(dst, src):
+            nc.vector.tensor_copy(
+                out=dst.rearrange("p (t m) -> p m t", t=PACK),
+                in_=src.rearrange("p (m t) -> p m t", t=PACK),
+            )
+
+        def deal_wb(g):
+            deal_bytes(wb_s[g][:], wb_s_raw[:].rearrange("p (a n) -> p a n", a=2)[:, :, g * PASS : (g + 1) * PASS])
+            for a in range(2):
+                deal_words(wb_w[a, g][:], wb_w_raw[g][:, a, :])
+
+        tanh_z = {}
+        for c in range(2):
+            v_s = sb([P, CHUNK], U8, "v_s%d" % c)
+            v2_s = sb([P, CHUNK], U8, "v2_s%d" % c, tag=("v2_s" if c == 0 else "wb_s_raw"))
+            v2_pairs = sb([P, CHUNK], U32, "v2_pairs%d" % c, tag=("v2_pairs" if c == 0 else "wb_w_raw1"))
+            v_w = sb([P, CHUNK], U32, "v_w%d" % c, tag=("v_w" if c == 0 else "wb_w_raw1"))
+            v2_w = sb([P, 2, CHUNK], U16, "v2_w%d" % c)
+
+            gather(v_s[:], tab_s[:], list1, c)
+            if c == 0:
+                deal_bytes(wa_s[:].rearrange("p (g n) -> p g n", g=2), wa_s_raw[:].rearrange("p (g n) -> p g n", g=2))
+                gather(v_w[:], tab_w[:].bitcast(U32), list1, c)
+                for g in range(2):
+                    deal_words(wa_w[g][:], wa_w_raw[:].bitcast(U16)[:, g * PASS : (g + 1) * PASS])
+            gather(v2_s[:], tab2_s[:], list2, c)
+            nc.gpsimd.dma_start(out=s2_second[c][0:LIVE, :].bitcast(I32), in_=v2_s[LIFT : LIFT + LIVE, :].bitcast(I32))
+            gather(v2_pairs[:], tab2_w[:].bitcast(U32), list2, c)
+            nc.vector.tensor_copy(out=v2_w[:], in_=v2_pairs[:].bitcast(U16).rearrange("p (j d) -> p d j", d=2))
+            if c == 0:
+                deal_wb(0)
+                deal_wb(1)
+            else:
+                gather(v_w[:], tab_w[:].bitcast(U32), list1, c)
+
+            groups = (0, 1) if c == 0 else (1, 0)
+            z = {(g, t): bank(PACK * n + t, "z%d_%d%d" % (c, g, t)) for n, g in enumerate(groups) for t in range(PACK)}
+
+            def wb_pass(a, g, t, start, stop):
+                cols = slice(t * P, (t + 1) * P)
+                plane = v2_s if a == 0 else s2_second[c]
+                nc.tensor.matmul_mx(
+                    out=z[g, t][:], lhsT=wb_w[a, g][:, cols].bitcast(FP8X4), lhsT_scale=wb_s[g][:, a, cols],
+                    rhs=v2_w[:, a, :].bitcast(FP4X4), rhs_scale=plane[:], start=start, stop=stop,
+                )
+
+            def wa_pass(g, t, start):
+                cols = slice(t * P, (t + 1) * P)
+                nc.tensor.matmul_mx(
+                    out=z[g, t][:], lhsT=wa_w[g][:, cols].bitcast(FP4X4), lhsT_scale=wa_s[:, g * PASS + t * P : g * PASS + (t + 1) * P],
+                    rhs=v_w[:].bitcast(FP8X4), rhs_scale=v_s[:], start=start, stop=False,
+                )
+
+            if c == 0:
+                for g in groups:
+                    for t in range(PACK):
+                        wa_pass(g, t, True)
+            for g in groups:
+                tanh_z[c, g] = sb([P, PACK, CHUNK], F32, "tanh_z%d%d" % (c, g))
+                for t in range(PACK):
+                    wb_pass(0, g, t, c == 1, False)
+                if c == 1:
+                    for t in range(PACK):
+                        wa_pass(g, t, False)
+                for t in range(PACK):
+                    wb_pass(1, g, t, False, True)
+                    nc.scalar.activation(out=tanh_z[c, g][:, t, :], in_=z[g, t][:], func=ACT.Tanh)
+
+        def scale_h(c, g, j0, width):
+            h = sb([P, width * PACK], BF16, "h%d%d_%d" % (c, g, j0))
+            nc.vector.tensor_tensor(
+                out=h[:].rearrange("p (u i t) -> p u t i", i=4, t=PACK),
+                in0=tanh_z[c, g][:, :, j0 : j0 + width].rearrange("p t (u i) -> p u t i", i=4),
+                in1=sm_t[:, g, :].unsqueeze(1).unsqueeze(3).to_broadcast([P, width // 4, PACK, 4]),
+                op=ALU.mult,
+            )
+            return h
+
+        def quantise_h(h, c, g, j0, width):
+            codes = sb([P, width], U32, "h_w%d%d_%d" % (c, g, j0))
+            plane = sb([P, width], U8, "h_s%d%d_%d" % (c, g, j0))
+            nc.vector.quantize_mx(out=codes[:].bitcast(FP8X4), scales=plane[:], in_=h[:])
+            return codes, plane
+
+        blocks = [(0, 0, 0, CHUNK), (0, 1, 0, CHUNK)] + [(1, g, j0, PIECE) for j0 in (0, PIECE) for g in (1, 0)]
+        hq = {}
+        pending = None
+        for blk in blocks:
+            h = scale_h(*blk)
+            if pending is not None:
+                hq[pending[1][:3]] = quantise_h(pending[0], *pending[1])
+            pending = (h, blk)
+        hq[pending[1][:3]] = quantise_h(pending[0], *pending[1])
+
+        def en8_pass(dst, m, codes, plane, start, stop):
+            cols = slice(m * P, (m + 1) * P)
+            nc.tensor.matmul_mx(out=dst, lhsT=en8_w[:, cols].bitcast(FP8X4), lhsT_scale=en8_s[:, cols],
+                                rhs=codes.bitcast(FP8X4), rhs_scale=plane, start=start, stop=stop)
+
+        def en4_pass(dst, m, codes, plane, start, stop):
+            nc.tensor.matmul_mx(out=dst, lhsT=en4_w[:, 2 * m * P : 2 * (m + 1) * P].bitcast(FP4X4),
+                                lhsT_scale=en4_s[:, m * P : (m + 1) * P],
+                                rhs=codes.bitcast(FP8X4), rhs_scale=plane, start=start, stop=stop)
+
+        def add_bias(on_vector, dst, src, m):
+            if on_vector:
+                nc.vector.tensor_scalar(out=dst, in0=src, scalar1=b_t[:, m : m + 1], scalar2=None, op0=ALU.add)
+            else:
+                nc.scalar.activation(out=dst, in_=src, func=ACT.Identity, bias=b_t[:, m : m + 1])
+
+        for m in range(N // P):
+            y = bank(m, "y0_%d" % m)
+            en8_pass(y[:], m, hq[0, 0, 0][0][:], hq[0, 0, 0][1][:], True, False)
+            en4_pass(y[:], m, hq[0, 1, 0][0][:], hq[0, 1, 0][1][:], False, True)
+            res = sb([P, CHUNK], F32, "res0_%d" % m)
+            add_bias(False, res[:], y[:], m)
+            nc.sync.dma_start(out=out[m * P : (m + 1) * P, 0:CHUNK], in_=res[:])
+
+        for piece in range(2):
+            j0 = piece * PIECE
+            for s in range(4):
+                y = bank(4 * piece + s, "y1_%d_%d" % (piece, s))
+                res = sb([P, 2, PIECE], F32, "res1_%d_%d" % (piece, s))
+                codes, plane = hq[1, 1, j0]
+                for e in range(2):
+                    for half in range(2):
+                        cols = slice(half * P, (half + 1) * P)
+                        dst = y[:, e * PIECE + half * P : e * PIECE + (half + 1) * P]
+                        en4_pass(dst, 2 * s + e, codes[:, cols], plane[:, cols], e == 0 and half == 0, False)
+                codes, plane = hq[1, 0, j0]
+                for e in range(2):
+                    en8_pass(y[:, e * PIECE : (e + 1) * PIECE], 2 * s + e, codes[:], plane[:], False, e == 1)
+                for e in range(2):
+                    add_bias(s % 2 == 1, res[:, e, :], y[:, e * PIECE : (e + 1) * PIECE], 2 * s + e)
+                rows = out[2 * s * P : 2 * (s + 1) * P, CHUNK + j0 : CHUNK + j0 + PIECE]
+                nc.sync.dma_start(out=rows.rearrange("(e p) j -> p e j", p=P), in_=res[:])

@@ -44,15 +44,11 @@ def tile_list_kg_tanh_mix_bias_kernel(
         def zero(tile_ap):
             nc.vector.memset(tile_ap.bitcast(I32), 0)
 
-        def load_plane(queues, plane, rows):
-            for q in range(QUADS):
-                queues[q].dma_start(out=plane[32 * q : 32 * q + 4, :].bitcast(I32), in_=rows[4 * q : 4 * q + 4, :].bitcast(I32))
-
-        def load_repeated(queues, plane, rows):
+        def load_repeated(plane, rows, quads):
             width = rows.shape[1] // 4
-            for q in range(QUADS):
+            for q in quads:
                 four = rows[4 * q : 4 * q + 4, :].bitcast(I32)
-                queues[q].dma_start(out=plane[32 * q : 32 * q + 32, :].bitcast(I32), in_=four.unsqueeze(0).to_broadcast([8, 4, width]))
+                nc.sync.dma_start(out=plane[32 * q : 32 * q + 32, :].bitcast(I32), in_=four.unsqueeze(0).to_broadcast([8, 4, width]))
 
         list1 = keep.tile([P, J // 16], U16, name="list1")
         list2 = keep.tile([P, J // 16], U16, name="list2")
@@ -64,46 +60,42 @@ def tile_list_kg_tanh_mix_bias_kernel(
         wa_s_raw = sb([P, R], U8, "wa_s_raw")
         wa_w_raw = sb([P, 2 * R], U8, "wa_w_raw")
         wb_s_raw = sb([P, 2 * R], U8, "wb_s_raw")
-        wb_w_raw = [sb([P, 2, PASS], I32, "wb_w_raw%d" % g) for g in range(2)]
-        en8_s = sb([P, N], U8, "en8_s")
-        en8_w = sb([P, N], I32, "en8_w")
-        en4_s = sb([P, N], U8, "en4_s")
-        en4_w = sb([P, 2 * N], U8, "en4_w")
+        wb_w_first = [sb([P, PASS], I32, "wb_w_first%d" % a) for a in range(2)]
+        wb_w_second = sb([P, 2, PASS], I32, "wb_w_second")
         sm_t = sb([P, 2, PACK], F32, "sm_t")
-        b_t = sb([P, N // P], F32, "b_t")
         s2_second = [sb([P, CHUNK], U8, "s2_second%d" % c) for c in range(2)]
 
-        for tl in (tab2_s, wb_s_raw, s2_second[0], s2_second[1], en8_s, en4_s):
+        for tl in (tab2_s, wb_s_raw, s2_second[0], s2_second[1]):
             zero(tl[:])
 
+        warm = sb([P, 8], F32, "warm")
+        nc.vector.memset(warm[:], 0.0)
+        nc.scalar.activation(out=warm[:, 4:8], in_=warm[:, 0:4], func=ACT.Tanh)
         nc.sync.dma_start(list1[:], offs)
-        load_repeated([nc.sync] * 4, tab_s, tab_scales[0])
-        load_repeated([nc.sync, nc.sync, nc.gpsimd, nc.gpsimd], wa_s_raw, wa_scales[0])
+        load_repeated(tab_s, tab_scales[0], range(4))
+        load_repeated(wa_s_raw, wa_scales[0], range(2))
         nc.sync.dma_start(out=tab_w[:], in_=tab_words[0].rearrange("p n t -> p (n t)").bitcast(I32))
+        load_repeated(wa_s_raw, wa_scales[0], range(2, 4))
         nc.sync.dma_start(out=wa_w_raw[:].bitcast(I32), in_=wa_words[0].bitcast(I32))
         nc.sync.dma_start(list2[:], offs2)
         for q in range(QUADS):
-            nc.sync.dma_start(out=tab2_s[32 * q : 32 * q + 8, :].bitcast(I32), in_=tab2_scales[:, 4 * q : 4 * q + 4, :].bitcast(I32))
+            queue = nc.sync if q < 2 else nc.gpsimd
+            queue.dma_start(out=tab2_s[32 * q : 32 * q + 8, :].bitcast(I32), in_=tab2_scales[:, 4 * q : 4 * q + 4, :].bitcast(I32))
         nc.sync.dma_start(out=tab2_w[:], in_=tab2_words[0].rearrange("p n t -> p (n t)").bitcast(I32))
         wb_rows = wb_words.rearrange("a p n t -> p a (n t)").bitcast(I32)
-        nc.sync.dma_start(out=wb_w_raw[0][:], in_=wb_rows[:, :, 0:PASS])
+        for a in range(2):
+            nc.sync.dma_start(out=wb_w_first[a][:], in_=wb_rows[:, a, 0:PASS])
         for q in range(QUADS):
             nc.sync.dma_start(
                 out=wb_s_raw[32 * q : 32 * q + 4, :].bitcast(I32).rearrange("p (a n) -> p a n", a=2),
                 in_=wb_scales[:, 4 * q : 4 * q + 4, :].bitcast(I32).rearrange("a r n -> r a n"),
             )
-        nc.sync.dma_start(out=wb_w_raw[1][:], in_=wb_rows[:, :, PASS : 2 * PASS])
+        nc.sync.dma_start(out=wb_w_second[:], in_=wb_rows[:, :, PASS : 2 * PASS])
         nc.sync.dma_start(out=sm_t[:], in_=sm.rearrange("(g p t) -> p g t", g=2, t=PACK))
-        nc.sync.dma_start(out=en8_w[:], in_=en8_words[0].rearrange("p n t -> p (n t)").bitcast(I32))
-        nc.sync.dma_start(out=en4_w[:].bitcast(I32), in_=en4_words[0].bitcast(I32))
-        load_plane([nc.sync] * 4, en8_s, en8_scales[0])
-        load_plane([nc.sync] * 4, en4_s, en4_scales[0])
-        with nc.allow_non_contiguous_dma(reason="one bias value a partition"):
-            nc.sync.dma_start(out=b_t[:], in_=b.rearrange("(m p) -> p m", p=P))
 
         wa_s = sb([P, R], U8, "wa_s")
         wa_w = [sb([P, PASS], U16, "wa_w%d" % g) for g in range(2)]
-        wb_s = [sb([P, 2, PASS], U8, "wb_s%d" % g) for g in range(2)]
+        wb_s = {}
         wb_w = {(a, g): sb([P, PASS], I32, "wb_w%d%d" % (a, g)) for g in range(2) for a in range(2)}
 
         def gather(dst, window, lst, c):
@@ -123,16 +115,17 @@ def tile_list_kg_tanh_mix_bias_kernel(
             )
 
         def deal_wb(g):
+            wb_s[g] = sb([P, 2, PASS], U8, "wb_s%d" % g, tag=("wb_s0" if g == 0 else "wb_w_first0"))
             deal_bytes(wb_s[g][:], wb_s_raw[:].rearrange("p (a n) -> p a n", a=2)[:, :, g * PASS : (g + 1) * PASS])
             for a in range(2):
-                deal_words(wb_w[a, g][:], wb_w_raw[g][:, a, :])
+                deal_words(wb_w[a, g][:], wb_w_first[a][:] if g == 0 else wb_w_second[:, a, :])
 
         tanh_z = {}
         for c in range(2):
             v_s = sb([P, CHUNK], U8, "v_s%d" % c)
             v2_s = sb([P, CHUNK], U8, "v2_s%d" % c, tag=("v2_s" if c == 0 else "wb_s_raw"))
-            v2_pairs = sb([P, CHUNK], U32, "v2_pairs%d" % c, tag=("v2_pairs" if c == 0 else "wb_w_raw1"))
-            v_w = sb([P, CHUNK], U32, "v_w%d" % c, tag=("v_w" if c == 0 else "wb_w_raw1"))
+            v2_pairs = sb([P, CHUNK], U32, "v2_pairs%d" % c, tag=("v2_pairs" if c == 0 else "wb_w_second"))
+            v_w = sb([P, CHUNK], U32, "v_w%d" % c, tag=("v_w" if c == 0 else "wb_w_second"))
             v2_w = sb([P, 2, CHUNK], U16, "v2_w%d" % c)
 
             gather(v_s[:], tab_s[:], list1, c)
@@ -142,7 +135,7 @@ def tile_list_kg_tanh_mix_bias_kernel(
                 for g in range(2):
                     deal_words(wa_w[g][:], wa_w_raw[:].bitcast(U16)[:, g * PASS : (g + 1) * PASS])
             gather(v2_s[:], tab2_s[:], list2, c)
-            nc.gpsimd.dma_start(out=s2_second[c][0:LIVE, :].bitcast(I32), in_=v2_s[LIFT : LIFT + LIVE, :].bitcast(I32))
+            (nc.scalar if c == 0 else nc.sync).dma_start(out=s2_second[c][0:LIVE, :].bitcast(I32), in_=v2_s[LIFT : LIFT + LIVE, :].bitcast(I32))
             gather(v2_pairs[:], tab2_w[:].bitcast(U32), list2, c)
             nc.vector.tensor_copy(out=v2_w[:], in_=v2_pairs[:].bitcast(U16).rearrange("p (j d) -> p d j", d=2))
             if c == 0:
@@ -183,6 +176,18 @@ def tile_list_kg_tanh_mix_bias_kernel(
                 for t in range(PACK):
                     wb_pass(1, g, t, False, True)
                     nc.scalar.activation(out=tanh_z[c, g][:, t, :], in_=z[g, t][:], func=ACT.Tanh)
+
+        en4_s = sb([P, N], U8, "en4_s", tag="wb_w_first1")
+        load_repeated(en4_s, en4_scales[0], range(4))
+        en8_s = sb([P, N], U8, "en8_s", tag="tab2_s")
+        load_repeated(en8_s, en8_scales[0], range(4))
+        en8_w = sb([P, N], I32, "en8_w", tag="tab2_w")
+        nc.sync.dma_start(out=en8_w[:], in_=en8_words[0].rearrange("p n t -> p (n t)").bitcast(I32))
+        en4_w = sb([P, 2 * N], U8, "en4_w", tag="tab_w")
+        nc.sync.dma_start(out=en4_w[:].bitcast(I32), in_=en4_words[0].bitcast(I32))
+        b_t = sb([P, N // P], F32, "b_t", tag="s2_second0")
+        with nc.allow_non_contiguous_dma(reason="one bias value a partition"):
+            nc.sync.dma_start(out=b_t[:], in_=b.rearrange("(m p) -> p m", p=P))
 
         def scale_h(c, g, j0, width):
             h = sb([P, width * PACK], BF16, "h%d%d_%d" % (c, g, j0))
@@ -234,21 +239,22 @@ def tile_list_kg_tanh_mix_bias_kernel(
             add_bias(False, res[:], y[:], m)
             nc.sync.dma_start(out=out[m * P : (m + 1) * P, 0:CHUNK], in_=res[:])
 
-        for piece in range(2):
+        shares = [(piece, (2 * s, 2 * s + 1)) for piece in range(2) for s in range(4)]
+        shares = shares[:-1] + [(1, (6,)), (1, (7,))]
+        for n, (piece, tiles) in enumerate(shares):
             j0 = piece * PIECE
-            for s in range(4):
-                y = bank(4 * piece + s, "y1_%d_%d" % (piece, s))
-                res = sb([P, 2, PIECE], F32, "res1_%d_%d" % (piece, s))
-                codes, plane = hq[1, 1, j0]
-                for e in range(2):
-                    for half in range(2):
-                        cols = slice(half * P, (half + 1) * P)
-                        dst = y[:, e * PIECE + half * P : e * PIECE + (half + 1) * P]
-                        en4_pass(dst, 2 * s + e, codes[:, cols], plane[:, cols], e == 0 and half == 0, False)
-                codes, plane = hq[1, 0, j0]
-                for e in range(2):
-                    en8_pass(y[:, e * PIECE : (e + 1) * PIECE], 2 * s + e, codes[:], plane[:], False, e == 1)
-                for e in range(2):
-                    add_bias(s % 2 == 1, res[:, e, :], y[:, e * PIECE : (e + 1) * PIECE], 2 * s + e)
-                rows = out[2 * s * P : 2 * (s + 1) * P, CHUNK + j0 : CHUNK + j0 + PIECE]
-                nc.sync.dma_start(out=rows.rearrange("(e p) j -> p e j", p=P), in_=res[:])
+            y = bank(n % 8, "y1_%d" % n)
+            res = sb([P, len(tiles), PIECE], F32, "res1_%d" % n)
+            codes, plane = hq[1, 1, j0]
+            for e, m in enumerate(tiles):
+                for half in range(2):
+                    cols = slice(half * P, (half + 1) * P)
+                    dst = y[:, e * PIECE + half * P : e * PIECE + (half + 1) * P]
+                    en4_pass(dst, m, codes[:, cols], plane[:, cols], e == 0 and half == 0, False)
+            codes, plane = hq[1, 0, j0]
+            for e, m in enumerate(tiles):
+                en8_pass(y[:, e * PIECE : (e + 1) * PIECE], m, codes[:], plane[:], False, e == len(tiles) - 1)
+            for e, m in enumerate(tiles):
+                add_bias(n % 2 == 1, res[:, e, :], y[:, e * PIECE : (e + 1) * PIECE], m)
+            rows = out[tiles[0] * P : (tiles[-1] + 1) * P, CHUNK + j0 : CHUNK + j0 + PIECE]
+            nc.sync.dma_start(out=rows.rearrange("(e p) j -> p e j", p=P), in_=res[:])

@@ -94,7 +94,7 @@ def tile_list_kg_tanh_mix_bias_kernel(
         nc.sync.dma_start(out=sm_t[:], in_=sm.rearrange("(g p t) -> p g t", g=2, t=PACK))
 
         wa_s = sb([P, R], U8, "wa_s")
-        wa_w = [sb([P, PASS], U16, "wa_w%d" % g) for g in range(2)]
+        wa_w = {}
         wb_s = {}
         wb_w = {(a, g): sb([P, PASS], I32, "wb_w%d%d" % (a, g)) for g in range(2) for a in range(2)}
 
@@ -110,8 +110,15 @@ def tile_list_kg_tanh_mix_bias_kernel(
 
         def deal_words(dst, src):
             nc.vector.tensor_copy(
-                out=dst.rearrange("p (t m) -> p m t", t=PACK),
-                in_=src.rearrange("p (m t) -> p m t", t=PACK),
+                out=dst.rearrange("p (th tl mo mi) -> p mo th mi tl", th=2, tl=2, mi=4),
+                in_=src.rearrange("p (mo mi th tl) -> p mo th mi tl", th=2, tl=2, mi=4),
+            )
+
+        def deal_wa(g):
+            wa_w[g] = sb([P, PASS], U16, "wa_w%d" % g)
+            halves = wa_w_raw[:].bitcast(U16)[:, g * PASS : (g + 1) * PASS]
+            nc.vector.tensor_copy(
+                out=wa_w[g][:].rearrange("p (t m) -> p t m", t=PACK), in_=halves.rearrange("p (m t) -> p t m", t=PACK)
             )
 
         def deal_wb(g):
@@ -132,8 +139,8 @@ def tile_list_kg_tanh_mix_bias_kernel(
             if c == 0:
                 deal_bytes(wa_s[:].rearrange("p (g n) -> p g n", g=2), wa_s_raw[:].rearrange("p (g n) -> p g n", g=2))
                 gather(v_w[:], tab_w[:].bitcast(U32), list1, c)
-                for g in range(2):
-                    deal_words(wa_w[g][:], wa_w_raw[:].bitcast(U16)[:, g * PASS : (g + 1) * PASS])
+                deal_wa(0)
+                deal_wa(1)
             gather(v2_s[:], tab2_s[:], list2, c)
             (nc.scalar if c == 0 else nc.sync).dma_start(out=s2_second[c][0:LIVE, :].bitcast(I32), in_=v2_s[LIFT : LIFT + LIVE, :].bitcast(I32))
             gather(v2_pairs[:], tab2_w[:].bitcast(U32), list2, c)
@@ -192,9 +199,9 @@ def tile_list_kg_tanh_mix_bias_kernel(
         def scale_h(c, g, j0, width):
             h = sb([P, width * PACK], BF16, "h%d%d_%d" % (c, g, j0))
             nc.vector.tensor_tensor(
-                out=h[:].rearrange("p (u i t) -> p u t i", i=4, t=PACK),
-                in0=tanh_z[c, g][:, :, j0 : j0 + width].rearrange("p t (u i) -> p u t i", i=4),
-                in1=sm_t[:, g, :].unsqueeze(1).unsqueeze(3).to_broadcast([P, width // 4, PACK, 4]),
+                out=h[:].rearrange("p (u i t) -> p u t i", i=2, t=PACK),
+                in0=tanh_z[c, g][:, :, j0 : j0 + width].rearrange("p t (u i) -> p u t i", i=2),
+                in1=sm_t[:, g, :].unsqueeze(1).unsqueeze(3).to_broadcast([P, width // 2, PACK, 2]),
                 op=ALU.mult,
             )
             return h

@@ -262,6 +262,6 @@ def tile_list_kg_tanh_mix_bias_kernel(
             for e, m in enumerate(tiles):
                 en8_pass(y[:, e * PIECE : (e + 1) * PIECE], m, codes[:], plane[:], False, e == len(tiles) - 1)
             for e, m in enumerate(tiles):
-                add_bias(n % 2 == 1, res[:, e, :], y[:, e * PIECE : (e + 1) * PIECE], m)
+                add_bias(piece == 1 and n % 2 == 1, res[:, e, :], y[:, e * PIECE : (e + 1) * PIECE], m)
             rows = out[tiles[0] * P : (tiles[-1] + 1) * P, CHUNK + j0 : CHUNK + j0 + PIECE]
             nc.sync.dma_start(out=rows.rearrange("(e p) j -> p e j", p=P), in_=res[:])

from contextlib import ExitStack

import concourse.mybir as mybir

K, L, R, N, T, J = 512, 1024, 1024, 1024, 2048, 1024
FLOPS = 2 * J * (K * R + L * R + R * N)

F32 = mybir.dt.float32
BF16 = mybir.dt.bfloat16
I32 = mybir.dt.int32
U32 = mybir.dt.uint32
U16 = mybir.dt.uint16
U8 = mybir.dt.uint8
FP8X4 = mybir.dt.float8_e4m3fn_x4
FP4X4 = mybir.dt.float4_e2m1fn_x4
ACT = mybir.ActivationFunctionType
ALU = mybir.AluOpType

P = 128
PACK = 4
PASS = P * PACK
CHUNK = 512
PIECE = 256
QUADS = 4
LIFT = 4
LIVE = 100


def tile_list_kg_tanh_mix_bias_kernel(
    tc, tab_words, tab_scales, tab2_words, tab2_scales, wa_words, wa_scales, wb_words, wb_scales,
    sm, en8_words, en8_scales, en4_words, en4_scales, b, offs, offs2, out,
):
    nc = tc.nc
    with ExitStack() as ctx:
        keep = ctx.enter_context(tc.tile_pool(name="keep", bufs=1))
        psum = ctx.enter_context(tc.psum_pool(name="psum", bufs=1))

        def sb(shape, dtype, name, tag=None):
            return keep.tile(shape, dtype, name=name, tag=tag or name, align_bytes=64)

        def bank(i, name):
            return psum.tile([P, 512], F32, name=name, tag="bank%d" % i)

        def zero(tile_ap):
            nc.vector.memset(tile_ap.bitcast(I32), 0)

        def load_repeated(plane, rows, quads):
            width = rows.shape[1] // 4
            for q in quads:
                four = rows[4 * q : 4 * q + 4, :].bitcast(I32)
                nc.sync.dma_start(out=plane[32 * q : 32 * q + 32, :].bitcast(I32), in_=four.unsqueeze(0).to_broadcast([8, 4, width]))

        list1 = keep.tile([P, J // 16], U16, name="list1")
        list2 = keep.tile([P, J // 16], U16, name="list2")

        tab_s = sb([P, T], U8, "tab_s")
        tab_w = sb([P, T], I32, "tab_w")
        tab2_s = sb([P, T], U8, "tab2_s")
        tab2_w = sb([P, T], I32, "tab2_w")
        wa_s_raw = sb([P, R], U8, "wa_s_raw")
        wa_w_raw = sb([P, 2 * R], U8, "wa_w_raw")
        wb_s_raw = sb([P, 2 * R], U8, "wb_s_raw")
        wb_w_first = [sb([P, PASS], I32, "wb_w_first%d" % a) for a in range(2)]
        wb_w_second = sb([P, 2, PASS], I32, "wb_w_second")
        sm_t = sb([P, 2, PACK], F32, "sm_t")
        s2_second = [sb([P, CHUNK], U8, "s2_second%d" % c) for c in range(2)]

        for tl in (tab2_s, wb_s_raw, s2_second[0], s2_second[1]):
            zero(tl[:])

        warm = sb([P, 8], F32, "warm")
        nc.vector.memset(warm[:], 0.0)
        nc.scalar.activation(out=warm[:, 4:8], in_=warm[:, 0:4], func=ACT.Tanh)
        nc.sync.dma_start(list1[:], offs)
        load_repeated(tab_s, tab_scales[0], range(4))
        load_repeated(wa_s_raw, wa_scales[0], range(2))
        nc.sync.dma_start(out=tab_w[:], in_=tab_words[0].rearrange("p n t -> p (n t)").bitcast(I32))
        load_repeated(wa_s_raw, wa_scales[0], range(2, 4))
        nc.sync.dma_start(out=wa_w_raw[:].bitcast(I32), in_=wa_words[0].bitcast(I32))
        nc.sync.dma_start(list2[:], offs2)
        for q in range(QUADS):
            queue = nc.sync if q < 2 else nc.gpsimd
            queue.dma_start(out=tab2_s[32 * q : 32 * q + 8, :].bitcast(I32), in_=tab2_scales[:, 4 * q : 4 * q + 4, :].bitcast(I32))
        nc.sync.dma_start(out=tab2_w[:], in_=tab2_words[0].rearrange("p n t -> p (n t)").bitcast(I32))
        wb_rows = wb_words.rearrange("a p n t -> p a (n t)").bitcast(I32)
        for a in range(2):
            nc.sync.dma_start(out=wb_w_first[a][:], in_=wb_rows[:, a, 0:PASS])
        for q in range(QUADS):
            nc.sync.dma_start(
                out=wb_s_raw[32 * q : 32 * q + 4, :].bitcast(I32).rearrange("p (a n) -> p a n", a=2),
                in_=wb_scales[:, 4 * q : 4 * q + 4, :].bitcast(I32).rearrange("a r n -> r a n"),
            )
        nc.sync.dma_start(out=wb_w_second[:], in_=wb_rows[:, :, PASS : 2 * PASS])
        nc.sync.dma_start(out=sm_t[:], in_=sm.rearrange("(g p t) -> p g t", g=2, t=PACK))

        wa_s = sb([P, R], U8, "wa_s")
        wa_w = {}
        wb_s = {}
        wb_w = {(a, g): sb([P, PASS], I32, "wb_w%d%d" % (a, g)) for g in range(2) for a in range(2)}

        def gather(dst, window, lst, c):
            cols = slice(c * CHUNK // 16, (c + 1) * CHUNK // 16)
            nc.vector.tensor_copy(dst, window.indirect(lst[:, cols]))

        def deal_bytes(dst, src):
            nc.vector.tensor_copy(
                out=dst.rearrange("p g (t m) -> p g t m", t=PACK),
                in_=src.rearrange("p g (m t) -> p g t m", t=PACK),
            )

        def deal_words(dst, src):
            nc.vector.tensor_copy(
                out=dst.rearrange("p (th tl mo mi) -> p mo th mi tl", th=2, tl=2, mi=4),
                in_=src.rearrange("p (mo mi th tl) -> p mo th mi tl", th=2, tl=2, mi=4),
            )

        def deal_wa(g):
            wa_w[g] = sb([P, PASS], U16, "wa_w%d" % g)
            halves = wa_w_raw[:].bitcast(U16)[:, g * PASS : (g + 1) * PASS]
            nc.vector.tensor_copy(
                out=wa_w[g][:].rearrange("p (t m) -> p t m", t=PACK), in_=halves.rearrange("p (m t) -> p t m", t=PACK)
            )

        def deal_wb(g):
            wb_s[g] = sb([P, 2, PASS], U8, "wb_s%d" % g, tag=("wb_s0" if g == 0 else "wb_w_first0"))
            deal_bytes(wb_s[g][:], wb_s_raw[:].rearrange("p (a n) -> p a n", a=2)[:, :, g * PASS : (g + 1) * PASS])
            for a in range(2):
                deal_words(wb_w[a, g][:], wb_w_first[a][:] if g == 0 else wb_w_second[:, a, :])

        tanh_z = {}
        for c in range(2):
            v_s = sb([P, CHUNK], U8, "v_s%d" % c)
            v2_s = sb([P, CHUNK], U8, "v2_s%d" % c, tag=("v2_s" if c == 0 else "wb_s_raw"))
            v2_pairs = sb([P, CHUNK], U32, "v2_pairs%d" % c, tag=("v2_pairs" if c == 0 else "wb_w_second"))
            v_w = sb([P, CHUNK], U32, "v_w%d" % c, tag=("v_w" if c == 0 else "wb_w_second"))
            v2_w = sb([P, 2, CHUNK], U16, "v2_w%d" % c)

            gather(v_s[:], tab_s[:], list1, c)
            if c == 0:
                deal_bytes(wa_s[:].rearrange("p (g n) -> p g n", g=2), wa_s_raw[:].rearrange("p (g n) -> p g n", g=2))
                gather(v_w[:], tab_w[:].bitcast(U32), list1, c)
                deal_wa(0)
                deal_wa(1)
            gather(v2_s[:], tab2_s[:], list2, c)
            (nc.scalar if c == 0 else nc.sync).dma_start(out=s2_second[c][0:LIVE, :].bitcast(I32), in_=v2_s[LIFT : LIFT + LIVE, :].bitcast(I32))
            gather(v2_pairs[:], tab2_w[:].bitcast(U32), list2, c)
            nc.vector.tensor_copy(out=v2_w[:], in_=v2_pairs[:].bitcast(U16).rearrange("p (j d) -> p d j", d=2))
            if c == 0:
                deal_wb(0)
                deal_wb(1)
            else:
                gather(v_w[:], tab_w[:].bitcast(U32), list1, c)

            groups = (0, 1) if c == 0 else (1, 0)
            z = {(g, t): bank(PACK * n + t, "z%d_%d%d" % (c, g, t)) for n, g in enumerate(groups) for t in range(PACK)}

            def wb_pass(a, g, t, start, stop):
                cols = slice(t * P, (t + 1) * P)
                plane = v2_s if a == 0 else s2_second[c]
                nc.tensor.matmul_mx(
                    out=z[g, t][:], lhsT=wb_w[a, g][:, cols].bitcast(FP8X4), lhsT_scale=wb_s[g][:, a, cols],
                    rhs=v2_w[:, a, :].bitcast(FP4X4), rhs_scale=plane[:], start=start, stop=stop,
                )

            def wa_pass(g, t, start):
                cols = slice(t * P, (t + 1) * P)
                nc.tensor.matmul_mx(
                    out=z[g, t][:], lhsT=wa_w[g][:, cols].bitcast(FP4X4), lhsT_scale=wa_s[:, g * PASS + t * P : g * PASS + (t + 1) * P],
                    rhs=v_w[:].bitcast(FP8X4), rhs_scale=v_s[:], start=start, stop=False,
                )

            if c == 0:
                for g in groups:
                    for t in range(PACK):
                        wa_pass(g, t, True)
            for g in groups:
                tanh_z[c, g] = sb([P, PACK, CHUNK], F32, "tanh_z%d%d" % (c, g))
                for t in range(PACK):
                    wb_pass(0, g, t, c == 1, False)
                if c == 1:
                    for t in range(PACK):
                        wa_pass(g, t, False)
                for t in range(PACK):
                    wb_pass(1, g, t, False, True)
                    nc.scalar.activation(out=tanh_z[c, g][:, t, :], in_=z[g, t][:], func=ACT.Tanh)

        en4_s = sb([P, N], U8, "en4_s", tag="wb_w_first1")
        load_repeated(en4_s, en4_scales[0], range(4))
        en8_s = sb([P, N], U8, "en8_s", tag="tab2_s")
        load_repeated(en8_s, en8_scales[0], range(4))
        en8_w = sb([P, N], I32, "en8_w", tag="tab2_w")
        nc.sync.dma_start(out=en8_w[:], in_=en8_words[0].rearrange("p n t -> p (n t)").bitcast(I32))
        en4_w = sb([P, 2 * N], U8, "en4_w", tag="tab_w")
        nc.sync.dma_start(out=en4_w[:].bitcast(I32), in_=en4_words[0].bitcast(I32))
        b_t = sb([P, N // P], F32, "b_t", tag="s2_second0")
        with nc.allow_non_contiguous_dma(reason="one bias value a partition"):
            nc.sync.dma_start(out=b_t[:], in_=b.rearrange("(m p) -> p m", p=P))

        def scale_h(c, g, j0, width):
            h = sb([P, width * PACK], BF16, "h%d%d_%d" % (c, g, j0))
            nc.vector.tensor_tensor(
                out=h[:].rearrange("p (u i t) -> p u t i", i=2, t=PACK),
                in0=tanh_z[c, g][:, :, j0 : j0 + width].rearrange("p t (u i) -> p u t i", i=2),
                in1=sm_t[:, g, :].unsqueeze(1).unsqueeze(3).to_broadcast([P, width // 2, PACK, 2]),
                op=ALU.mult,
            )
            return h

        def quantise_h(h, c, g, j0, width):
            codes = sb([P, width], U32, "h_w%d%d_%d" % (c, g, j0))
            plane = sb([P, width], U8, "h_s%d%d_%d" % (c, g, j0))
            nc.vector.quantize_mx(out=codes[:].bitcast(FP8X4), scales=plane[:], in_=h[:])
            return codes, plane

        blocks = [(0, 0, 0, CHUNK), (0, 1, 0, CHUNK)] + [(1, g, j0, PIECE) for j0 in (0, PIECE) for g in (1, 0)]
        hq = {}
        pending = None
        for blk in blocks:
            h = scale_h(*blk)
            if pending is not None:
                hq[pending[1][:3]] = quantise_h(pending[0], *pending[1])
            pending = (h, blk)
        hq[pending[1][:3]] = quantise_h(pending[0], *pending[1])

        def en8_pass(dst, m, codes, plane, start, stop):
            cols = slice(m * P, (m + 1) * P)
            nc.tensor.matmul_mx(out=dst, lhsT=en8_w[:, cols].bitcast(FP8X4), lhsT_scale=en8_s[:, cols],
                                rhs=codes.bitcast(FP8X4), rhs_scale=plane, start=start, stop=stop)

        def en4_pass(dst, m, codes, plane, start, stop):
            nc.tensor.matmul_mx(out=dst, lhsT=en4_w[:, 2 * m * P : 2 * (m + 1) * P].bitcast(FP4X4),
                                lhsT_scale=en4_s[:, m * P : (m + 1) * P],
                                rhs=codes.bitcast(FP8X4), rhs_scale=plane, start=start, stop=stop)

        def add_bias(on_vector, dst, src, m):
            if on_vector:
                nc.vector.tensor_scalar(out=dst, in0=src, scalar1=b_t[:, m : m + 1], scalar2=None, op0=ALU.add)
            else:
                nc.scalar.activation(out=dst, in_=src, func=ACT.Identity, bias=b_t[:, m : m + 1])

        for m in range(N // P):
            y = bank(m, "y0_%d" % m)
            en8_pass(y[:], m, hq[0, 0, 0][0][:], hq[0, 0, 0][1][:], True, False)
            en4_pass(y[:], m, hq[0, 1, 0][0][:], hq[0, 1, 0][1][:], False, True)
            res = sb([P, CHUNK], F32, "res0_%d" % m)
            add_bias(False, res[:], y[:], m)
            nc.sync.dma_start(out=out[m * P : (m + 1) * P, 0:CHUNK], in_=res[:])

        shares = [(piece, (2 * s, 2 * s + 1)) for piece in range(2) for s in range(4)]
        shares = shares[:-1] + [(1, (6,)), (1, (7,))]
        for n, (piece, tiles) in enumerate(shares):
            j0 = piece * PIECE
            y = bank(n % 8, "y1_%d" % n)
            res = sb([P, len(tiles), PIECE], F32, "res1_%d" % n)
            codes, plane = hq[1, 1, j0]
            for e, m in enumerate(tiles):
                for half in range(2):
                    cols = slice(half * P, (half + 1) * P)
                    dst = y[:, e * PIECE + half * P : e * PIECE + (half + 1) * P]
                    en4_pass(dst, m, codes[:, cols], plane[:, cols], e == 0 and half == 0, False)
            codes, plane = hq[1, 0, j0]
            for e, m in enumerate(tiles):
                en8_pass(y[:, e * PIECE : (e + 1) * PIECE], m, codes[:], plane[:], False, e == len(tiles) - 1)
            for e, m in enumerate(tiles):
                add_bias(piece == 1 and n % 2 == 1, res[:, e, :], y[:, e * PIECE : (e + 1) * PIECE], m)
            rows = out[tiles[0] * P : (tiles[-1] + 1) * P, CHUNK + j0 : CHUNK + j0 + PIECE]
            nc.sync.dma_start(out=rows.rearrange("(e p) j -> p e j", p=P), in_=res[:])
